import numpy as np, ml_dtypes
CORES = [83,85,87,115,117,119]
N = 6
WB, KB, QP = 2, 2, 256
def setup_inputs(rng):
    return {"q": rng.standard_normal((N, 128, QP), dtype=np.float32).astype(ml_dtypes.bfloat16), "k": rng.standard_normal((N, 128, KB * 128), dtype=np.float32).astype(ml_dtypes.bfloat16), "v": rng.standard_normal((N, 128, KB * 128), dtype=np.float32).astype(ml_dtypes.bfloat16)}
def setup_inputs_big(rng):
    d = setup_inputs(rng)
    for k in ("q", "k", "v"): d[k] = (d[k].astype(np.float32) * 1024.0).astype(d[k].dtype)
    return d
def setup_inputs_small(rng):
    d = setup_inputs(rng)
    for k in ("q", "k", "v"): d[k] = (d[k].astype(np.float32) * (1 / 1024.0)).astype(d[k].dtype)
    return d
def setup_inputs_apart(rng):
    d = setup_inputs(rng)
    f = (10.0 ** rng.permutation(np.linspace(-1.5, 1.5, N))).astype(np.float32).reshape(N, 1, 1)
    for k in ("q", "k", "v"): d[k] = (d[k].astype(np.float32) * f).astype(d[k].dtype)
    return d
def reference(q, k, v):
    Q, K, V = q.astype(np.float64), k.astype(np.float64), v.astype(np.float64)
    y = np.zeros((N, 128, QP))
    for r in range(N):
        for j in range(max(0, r - WB), r + 1):
            for b in range(KB):
                S = np.maximum(K[j][:, 128 * b:128 * b + 128].T @ Q[r], 0.0)
                y[r] += V[j][:, 128 * b:128 * b + 128].T @ S
    return {"y": y.astype(ml_dtypes.bfloat16 if q.dtype != np.float64 else np.float64)}

@@ -1,0 +1,115 @@
+from concourse.bass import DstId, RemoteDMATransfer
+from concourse.mybir import AluOpType
+
+WB, KB, QP, P = 2, 2, 256, 128
+NBLK = (WB + 1) * KB
+WIDTH = 8
+
+SCRATCH = {
+    "qs": ("sbuf", [P, QP], "bfloat16"),
+    "kv0": ("sbuf", [P, 2 * KB * P], "bfloat16"),
+    "kv1": ("sbuf", [P, 2 * KB * P], "bfloat16"),
+    "kv2": ("sbuf", [P, 2 * KB * P], "bfloat16"),
+    "zero": ("sbuf", [P, QP], "float32"),
+    "ys": ("sbuf", [P, QP], "bfloat16"),
+    "po": ("psum", [P, 512], "float32"),
+}
+for _i in range(NBLK):
+    SCRATCH["s%d" % _i] = ("sbuf", [P, QP], "bfloat16")
+    SCRATCH["ps%d" % _i] = ("psum", [P, 512], "float32")
+
+SEMAPHORES = ["ld_kv", "ld_q", "zs", "arr1", "arr2", "sent", "od", "yc", "st"] \
+    + ["mm%d" % _i for _i in range(NBLK)] + ["rl%d" % _i for _i in range(NBLK)]
+
+
+def _bits(mask):
+    return [b for b in range(mask.bit_length()) if (mask >> b) & 1]
+
+
+def _plan(cores, topo):
+    n = len(cores)
+    plan = []
+    for j in range(n):
+        src = cores[j]
+        dsts = [d for d in range(j + 1, min(j + WB, n - 1) + 1)]
+        far = [d for d in dsts if topo.chip(cores[d]) != topo.chip(src)]
+        near = [d for d in dsts if d not in far]
+        calls, used = [], []
+        for group in (far, near):
+            if not group:
+                continue
+            eng = [b for b in _bits(topo.mask(src, cores[group[0]])) if b not in used]
+            share = min(WIDTH, len(eng) // len(group))
+            calls.append([(d, eng[i * share:(i + 1) * share]) for i, d in enumerate(group)])
+            used = used + eng[:share * len(group)]
+        plan.append(calls)
+    return plan
+
+
+def rank_program(g, core, T, topo):
+    r = T.rank_of(core)
+    if r is None:
+        return
+    cores = T.cores
+    plan = _plan(cores, topo)
+    sem = T.sem
+    KW = KB * P
+
+    g.sync.dma_start(T.kv0[:, 0:KW], T.k[:]).then_inc(sem.ld_kv, 16)
+    g.scalar.dma_start(T.kv0[:, KW:2 * KW], T.v[:]).then_inc(sem.ld_kv, 16)
+    g.sync.dma_start(T.qs[:], T.q[:]).then_inc(sem.ld_q, 16)
+
+    if plan[r]:
+        g.wait_ge(sem.ld_kv, 32)
+        total = 0
+        for call in plan[r]:
+            trs = []
+            for d, eng in call:
+                rid, pid, _se = topo.addr(cores[d])
+                trs.append(RemoteDMATransfer(
+                    dst_ids=[DstId(rid=rid, pnc=pid)], dma_engine_mask=sum(1 << b for b in eng),
+                    remote_sem=sem["arr%d" % (d - r)], src=T.kv0[:], dst=T["kv%d" % (d - r)][:]))
+                total += len(eng)
+            g.remote_dma_fused(trs, local_sem=sem.sent)
+        g.wait_ge(sem.sent, total)
+
+    srcs = []
+    for j in range(max(0, r - WB), r):
+        for ci, call in enumerate(plan[j]):
+            for d, eng in call:
+                if d == r:
+                    srcs.append((P // len(eng), ci, r - j, len(eng)))
+    srcs.sort()
+    work = [(0, 0)] + [(dist, cnt) for _rows, _ci, dist, cnt in srcs]
+    nblk = len(work) * KB
+
+    g.vector.memset(T.zero[:], 0.0).then_inc(sem.zs, 1)
+    g.vector.wait_ge(sem.zs, 1)
+
+    i = 0
+    for dist, cnt in work:
+        kv = T["kv%d" % dist]
+        if dist == 0:
+            g.tensor.wait_ge(sem.ld_kv, 32)
+            g.tensor.wait_ge(sem.ld_q, 16)
+        else:
+            g.tensor.wait_ge(sem["arr%d" % dist], cnt)
+        for b in range(KB):
+            g.tensor.matmul(T["ps%d" % (i + b)][:, 0:QP], kv[:, b * P:(b + 1) * P], T.qs[:],
+                            start=True, stop=True).then_inc(sem["mm%d" % (i + b)], 1)
+            g.vector.wait_ge(sem["mm%d" % (i + b)], 1)
+            g.vector.tensor_tensor(T["s%d" % (i + b)][:], T["ps%d" % (i + b)][:, 0:QP], T.zero[:],
+                                   AluOpType.max).then_inc(sem["rl%d" % (i + b)], 1)
+        for b in range(KB):
+            g.tensor.wait_ge(sem["rl%d" % (i + b)], 1)
+            mm = g.tensor.matmul(T.po[:, 0:QP], kv[:, KW + b * P:KW + (b + 1) * P], T["s%d" % (i + b)][:],
+                                 start=(i + b == 0), stop=(i + b == nblk - 1))
+            if i + b == nblk - 1:
+                mm.then_inc(sem.od, 1)
+        i += KB
+
+    g.vector.wait_ge(sem.od, 1)
+    g.vector.tensor_copy(T.ys[:], T.po[:, 0:QP]).then_inc(sem.yc, 1)
+    g.sync.wait_ge(sem.yc, 1)
+    g.sync.dma_start(T.y[:], T.ys[:]).then_inc(sem.st, 16)
+    g.sync.wait_ge(sem.st, 16)

@@ -3,22 +3,27 @@ from concourse.mybir import AluOpType
 
 WB, KB, QP, P = 2, 2, 256, 128
 NBLK = (WB + 1) * KB
+KW = KB * P
+HQ = QP // 2
 WIDTH = 8
+FORWARD = True
 
 SCRATCH = {
     "qs": ("sbuf", [P, QP], "bfloat16"),
-    "kv0": ("sbuf", [P, 2 * KB * P], "bfloat16"),
-    "kv1": ("sbuf", [P, 2 * KB * P], "bfloat16"),
-    "kv2": ("sbuf", [P, 2 * KB * P], "bfloat16"),
     "zero": ("sbuf", [P, QP], "float32"),
     "ys": ("sbuf", [P, QP], "bfloat16"),
-    "po": ("psum", [P, 512], "float32"),
+    "poa": ("psum", [P, 512], "float32"),
+    "pob": ("psum", [P, 512], "float32"),
 }
+for _d in range(WB + 1):
+    SCRATCH["k%d" % _d] = ("sbuf", [P, KW], "bfloat16")
+    SCRATCH["v%d" % _d] = ("sbuf", [P, KW], "bfloat16")
 for _i in range(NBLK):
     SCRATCH["s%d" % _i] = ("sbuf", [P, QP], "bfloat16")
     SCRATCH["ps%d" % _i] = ("psum", [P, 512], "float32")
 
-SEMAPHORES = ["ld_kv", "ld_q", "zs", "arr1", "arr2", "sent", "od", "yc", "st"] \
+SEMAPHORES = ["ld_k", "ld_v", "ld_q", "zs", "sent", "oda", "odb", "yc", "st"] \
+    + ["a%s%d" % (_p, _d) for _p in "kv" for _d in range(1, WB + 1)] \
     + ["mm%d" % _i for _i in range(NBLK)] + ["rl%d" % _i for _i in range(NBLK)]
 
 
@@ -26,24 +31,40 @@ def _bits(mask):
     return [b for b in range(mask.bit_length()) if (mask >> b) & 1]
 
 
+def _pow2(n):
+    p = 1
+    while p * 2 <= n:
+        p *= 2
+    return p
+
+
 def _plan(cores, topo):
     n = len(cores)
-    plan = []
+    direct, forward, way = {}, dict((s, []) for s in range(n)), {}
     for j in range(n):
-        src = cores[j]
-        dsts = [d for d in range(j + 1, min(j + WB, n - 1) + 1)]
-        far = [d for d in dsts if topo.chip(cores[d]) != topo.chip(src)]
+        dsts = list(range(j + 1, min(j + WB, n - 1) + 1))
+        far = [d for d in dsts if topo.chip(cores[d]) != topo.chip(cores[j])]
         near = [d for d in dsts if d not in far]
-        calls, used = [], []
-        for group in (far, near):
+        if FORWARD and len(far) > 1 and len(set(topo.chip(cores[d]) for d in far)) == 1:
+            head = ([d for d in far if topo.die(cores[d]) == topo.die(cores[j])] or far)[0]
+            forward[head] += [(j, d) for d in far if d != head]
+            far = [head]
+        direct[j] = (far, near)
+    for s in range(n):
+        used = []
+        for kind, group in ((2, direct[s][0]), (1, direct[s][1])):
             if not group:
                 continue
-            eng = [b for b in _bits(topo.mask(src, cores[group[0]])) if b not in used]
-            share = min(WIDTH, len(eng) // len(group))
-            calls.append([(d, eng[i * share:(i + 1) * share]) for i, d in enumerate(group)])
-            used = used + eng[:share * len(group)]
-        plan.append(calls)
-    return plan
+            free = [b for b in _bits(topo.mask(cores[s], cores[group[0]])) if b not in used]
+            share = min(WIDTH, _pow2(len(free) // len(group)))
+            for i, d in enumerate(group):
+                way[(s, d)] = (free[i * share:(i + 1) * share], kind)
+            used += free[:share * len(group)]
+        for j, d in forward[s]:
+            ok = _bits(topo.mask(cores[s], cores[d]))
+            pref = [b for b in used if b in ok] + [b for b in ok if b not in used]
+            way[(j, d)] = (pref[:WIDTH], 3)
+    return direct, forward, way
 
 
 def rank_program(g, core, T, topo):
@@ -51,65 +72,103 @@ def rank_program(g, core, T, topo):
     if r is None:
         return
     cores = T.cores
-    plan = _plan(cores, topo)
+    direct, forward, way = _plan(cores, topo)
     sem = T.sem
-    KW = KB * P
 
-    g.sync.dma_start(T.kv0[:, 0:KW], T.k[:]).then_inc(sem.ld_kv, 16)
-    g.scalar.dma_start(T.kv0[:, KW:2 * KW], T.v[:]).then_inc(sem.ld_kv, 16)
-    g.sync.dma_start(T.qs[:], T.q[:]).then_inc(sem.ld_q, 16)
+    g.sync.dma_start(T.k0[:], T.k[:]).then_inc(sem.ld_k, 16)
+    g.scalar.dma_start(T.qs[:], T.q[:]).then_inc(sem.ld_q, 16)
+    g.sync.dma_start(T.v0[:], T.v[:]).then_inc(sem.ld_v, 16)
 
-    if plan[r]:
-        g.wait_ge(sem.ld_kv, 32)
-        total = 0
-        for call in plan[r]:
-            trs = []
-            for d, eng in call:
-                rid, pid, _se = topo.addr(cores[d])
-                trs.append(RemoteDMATransfer(
-                    dst_ids=[DstId(rid=rid, pnc=pid)], dma_engine_mask=sum(1 << b for b in eng),
-                    remote_sem=sem["arr%d" % (d - r)], src=T.kv0[:], dst=T["kv%d" % (d - r)][:]))
-                total += len(eng)
-            g.remote_dma_fused(trs, local_sem=sem.sent)
-        g.wait_ge(sem.sent, total)
+    total = [0]
 
-    srcs = []
-    for j in range(max(0, r - WB), r):
-        for ci, call in enumerate(plan[j]):
-            for d, eng in call:
-                if d == r:
-                    srcs.append((P // len(eng), ci, r - j, len(eng)))
-    srcs.sort()
-    work = [(0, 0)] + [(dist, cnt) for _rows, _ci, dist, cnt in srcs]
-    nblk = len(work) * KB
+    def send(part, origin, group):
+        trs = []
+        for d in group:
+            rid, pid, _se = topo.addr(cores[d])
+            eng = way[(origin, d)][0]
+            trs.append(RemoteDMATransfer(
+                dst_ids=[DstId(rid=rid, pnc=pid)], dma_engine_mask=sum(1 << b for b in eng),
+                remote_sem=sem["a%s%d" % (part, d - origin)],
+                src=T["%s%d" % (part, r - origin)][:], dst=T["%s%d" % (part, d - origin)][:]))
+            total[0] += len(eng)
+        g.remote_dma_fused(trs, local_sem=sem.sent)
+
+    for part in "kv":
+        if direct[r][0] or direct[r][1]:
+            g.wait_ge(sem["ld_" + part], 16)
+        for group in direct[r]:
+            if group:
+                send(part, r, group)
+    for part in "kv":
+        for j, d in forward[r]:
+            g.wait_ge(sem["a%s%d" % (part, r - j)], len(way[(j, r)][0]))
+            send(part, j, [d])
+    if total[0]:
+        g.wait_ge(sem.sent, total[0])
+
+    srcs = sorted((way[(j, r)][1], r - j) for j in range(max(0, r - WB), r))
+    groups = [[0]]
+    last_kind = 0
+    for kind, dist in srcs:
+        if kind == last_kind:
+            groups[-1].append(dist)
+        else:
+            groups.append([dist])
+        last_kind = kind
+    nblk = (len(srcs) + 1) * KB
+    final = groups[-1][-1]
 
     g.vector.memset(T.zero[:], 0.0).then_inc(sem.zs, 1)
     g.vector.wait_ge(sem.zs, 1)
 
-    i = 0
-    for dist, cnt in work:
-        kv = T["kv%d" % dist]
+    def arrived(part, dist):
         if dist == 0:
-            g.tensor.wait_ge(sem.ld_kv, 32)
-            g.tensor.wait_ge(sem.ld_q, 16)
+            g.tensor.wait_ge(sem["ld_" + part], 16)
         else:
-            g.tensor.wait_ge(sem["arr%d" % dist], cnt)
-        for b in range(KB):
-            g.tensor.matmul(T["ps%d" % (i + b)][:, 0:QP], kv[:, b * P:(b + 1) * P], T.qs[:],
-                            start=True, stop=True).then_inc(sem["mm%d" % (i + b)], 1)
-            g.vector.wait_ge(sem["mm%d" % (i + b)], 1)
-            g.vector.tensor_tensor(T["s%d" % (i + b)][:], T["ps%d" % (i + b)][:, 0:QP], T.zero[:],
-                                   AluOpType.max).then_inc(sem["rl%d" % (i + b)], 1)
-        for b in range(KB):
-            g.tensor.wait_ge(sem["rl%d" % (i + b)], 1)
-            mm = g.tensor.matmul(T.po[:, 0:QP], kv[:, KW + b * P:KW + (b + 1) * P], T["s%d" % (i + b)][:],
-                                 start=(i + b == 0), stop=(i + b == nblk - 1))
-            if i + b == nblk - 1:
-                mm.then_inc(sem.od, 1)
-        i += KB
+            g.tensor.wait_ge(sem["a%s%d" % (part, dist)], len(way[(r - dist, r)][0]))
 
-    g.vector.wait_ge(sem.od, 1)
-    g.vector.tensor_copy(T.ys[:], T.po[:, 0:QP]).then_inc(sem.yc, 1)
-    g.sync.wait_ge(sem.yc, 1)
+    done = {"a": 0, "b": 0}
+
+    def o_half(h, dist, b, i):
+        po, c0 = (T.poa, 0) if h == "a" else (T.pob, HQ)
+        mm = g.tensor.matmul(po[:, 0:HQ], T["v%d" % dist][:, b * P:(b + 1) * P], T["s%d" % i][:, c0:c0 + HQ],
+                             start=(done[h] == 0), stop=(done[h] == nblk - 1))
+        done[h] += 1
+        if done[h] == nblk:
+            mm.then_inc(sem["od" + h], 1)
+
+    i = 0
+    g.tensor.wait_ge(sem.ld_q, 16)
+    for group in groups:
+        first = i
+        for dist in group:
+            arrived("k", dist)
+            for b in range(KB):
+                g.tensor.matmul(T["ps%d" % i][:, 0:QP], T["k%d" % dist][:, b * P:(b + 1) * P], T.qs[:],
+                                start=True, stop=True).then_inc(sem["mm%d" % i], 1)
+                g.vector.wait_ge(sem["mm%d" % i], 1)
+                g.vector.tensor_tensor(T["s%d" % i][:], T["ps%d" % i][:, 0:QP], T.zero[:],
+                                       AluOpType.max).then_inc(sem["rl%d" % i], 1)
+                i += 1
+        i = first
+        for dist in group:
+            arrived("v", dist)
+            if dist == final:
+                order = [(h, b) for h in "ab" for b in range(KB)]
+            else:
+                order = [(h, b) for b in range(KB) for h in "ab"]
+            seen = []
+            for h, b in order:
+                if b not in seen:
+                    g.tensor.wait_ge(sem["rl%d" % (i + b)], 1)
+                    seen.append(b)
+                o_half(h, dist, b, i + b)
+            i += KB
+
+    g.vector.wait_ge(sem.oda, 1)
+    g.vector.tensor_copy(T.ys[:, 0:HQ], T.poa[:, 0:HQ]).then_inc(sem.yc, 1)
+    g.vector.wait_ge(sem.odb, 1)
+    g.vector.tensor_copy(T.ys[:, HQ:QP], T.pob[:, 0:HQ]).then_inc(sem.yc, 1)
+    g.sync.wait_ge(sem.yc, 2)
     g.sync.dma_start(T.y[:], T.ys[:]).then_inc(sem.st, 16)
     g.sync.wait_ge(sem.st, 16)

from concourse.bass import DstId, RemoteDMATransfer
from concourse.mybir import AluOpType

WB, KB, QP, P = 2, 2, 256, 128
NBLK = (WB + 1) * KB
KW = KB * P
HQ = QP // 2
WIDTH = 8
FORWARD = True

SCRATCH = {
    "qs": ("sbuf", [P, QP], "bfloat16"),
    "zero": ("sbuf", [P, QP], "float32"),
    "ys": ("sbuf", [P, QP], "bfloat16"),
    "poa": ("psum", [P, 512], "float32"),
    "pob": ("psum", [P, 512], "float32"),
}
for _d in range(WB + 1):
    SCRATCH["k%d" % _d] = ("sbuf", [P, KW], "bfloat16")
    SCRATCH["v%d" % _d] = ("sbuf", [P, KW], "bfloat16")
for _i in range(NBLK):
    SCRATCH["s%d" % _i] = ("sbuf", [P, QP], "bfloat16")
    SCRATCH["ps%d" % _i] = ("psum", [P, 512], "float32")

SEMAPHORES = ["ld_k", "ld_v", "ld_q", "zs", "sent", "oda", "odb", "yc", "st"] \
    + ["a%s%d" % (_p, _d) for _p in "kv" for _d in range(1, WB + 1)] \
    + ["mm%d" % _i for _i in range(NBLK)] + ["rl%d" % _i for _i in range(NBLK)]


def _bits(mask):
    return [b for b in range(mask.bit_length()) if (mask >> b) & 1]


def _pow2(n):
    p = 1
    while p * 2 <= n:
        p *= 2
    return p


def _plan(cores, topo):
    n = len(cores)
    direct, forward, way = {}, dict((s, []) for s in range(n)), {}
    for j in range(n):
        dsts = list(range(j + 1, min(j + WB, n - 1) + 1))
        far = [d for d in dsts if topo.chip(cores[d]) != topo.chip(cores[j])]
        near = [d for d in dsts if d not in far]
        if FORWARD and len(far) > 1 and len(set(topo.chip(cores[d]) for d in far)) == 1:
            head = ([d for d in far if topo.die(cores[d]) == topo.die(cores[j])] or far)[0]
            forward[head] += [(j, d) for d in far if d != head]
            far = [head]
        direct[j] = (far, near)
    for s in range(n):
        used = []
        for kind, group in ((2, direct[s][0]), (1, direct[s][1])):
            if not group:
                continue
            free = [b for b in _bits(topo.mask(cores[s], cores[group[0]])) if b not in used]
            share = min(WIDTH, _pow2(len(free) // len(group)))
            for i, d in enumerate(group):
                way[(s, d)] = (free[i * share:(i + 1) * share], kind)
            used += free[:share * len(group)]
        for j, d in forward[s]:
            ok = _bits(topo.mask(cores[s], cores[d]))
            pref = [b for b in used if b in ok] + [b for b in ok if b not in used]
            way[(j, d)] = (pref[:WIDTH], 3)
    return direct, forward, way


def rank_program(g, core, T, topo):
    r = T.rank_of(core)
    if r is None:
        return
    cores = T.cores
    direct, forward, way = _plan(cores, topo)
    sem = T.sem

    g.sync.dma_start(T.k0[:], T.k[:]).then_inc(sem.ld_k, 16)
    g.scalar.dma_start(T.qs[:], T.q[:]).then_inc(sem.ld_q, 16)
    g.sync.dma_start(T.v0[:], T.v[:]).then_inc(sem.ld_v, 16)

    total = [0]

    def send(part, origin, group):
        trs = []
        for d in group:
            rid, pid, _se = topo.addr(cores[d])
            eng = way[(origin, d)][0]
            trs.append(RemoteDMATransfer(
                dst_ids=[DstId(rid=rid, pnc=pid)], dma_engine_mask=sum(1 << b for b in eng),
                remote_sem=sem["a%s%d" % (part, d - origin)],
                src=T["%s%d" % (part, r - origin)][:], dst=T["%s%d" % (part, d - origin)][:]))
            total[0] += len(eng)
        g.remote_dma_fused(trs, local_sem=sem.sent)

    for part in "kv":
        if direct[r][0] or direct[r][1]:
            g.wait_ge(sem["ld_" + part], 16)
        for group in direct[r]:
            if group:
                send(part, r, group)
    for part in "kv":
        for j, d in forward[r]:
            g.wait_ge(sem["a%s%d" % (part, r - j)], len(way[(j, r)][0]))
            send(part, j, [d])
    if total[0]:
        g.wait_ge(sem.sent, total[0])

    srcs = sorted((way[(j, r)][1], r - j) for j in range(max(0, r - WB), r))
    groups = [[0]]
    last_kind = 0
    for kind, dist in srcs:
        if kind == last_kind:
            groups[-1].append(dist)
        else:
            groups.append([dist])
        last_kind = kind
    nblk = (len(srcs) + 1) * KB
    final = groups[-1][-1]

    g.vector.memset(T.zero[:], 0.0).then_inc(sem.zs, 1)
    g.vector.wait_ge(sem.zs, 1)

    def arrived(part, dist):
        if dist == 0:
            g.tensor.wait_ge(sem["ld_" + part], 16)
        else:
            g.tensor.wait_ge(sem["a%s%d" % (part, dist)], len(way[(r - dist, r)][0]))

    done = {"a": 0, "b": 0}

    def o_half(h, dist, b, i):
        po, c0 = (T.poa, 0) if h == "a" else (T.pob, HQ)
        mm = g.tensor.matmul(po[:, 0:HQ], T["v%d" % dist][:, b * P:(b + 1) * P], T["s%d" % i][:, c0:c0 + HQ],
                             start=(done[h] == 0), stop=(done[h] == nblk - 1))
        done[h] += 1
        if done[h] == nblk:
            mm.then_inc(sem["od" + h], 1)

    i = 0
    g.tensor.wait_ge(sem.ld_q, 16)
    for group in groups:
        first = i
        for dist in group:
            arrived("k", dist)
            for b in range(KB):
                g.tensor.matmul(T["ps%d" % i][:, 0:QP], T["k%d" % dist][:, b * P:(b + 1) * P], T.qs[:],
                                start=True, stop=True).then_inc(sem["mm%d" % i], 1)
                g.vector.wait_ge(sem["mm%d" % i], 1)
                g.vector.tensor_tensor(T["s%d" % i][:], T["ps%d" % i][:, 0:QP], T.zero[:],
                                       AluOpType.max).then_inc(sem["rl%d" % i], 1)
                i += 1
        i = first
        for dist in group:
            arrived("v", dist)
            if dist == final:
                order = [(h, b) for h in "ab" for b in range(KB)]
            else:
                order = [(h, b) for b in range(KB) for h in "ab"]
            seen = []
            for h, b in order:
                if b not in seen:
                    g.tensor.wait_ge(sem["rl%d" % (i + b)], 1)
                    seen.append(b)
                o_half(h, dist, b, i + b)
            i += KB

    g.vector.wait_ge(sem.oda, 1)
    g.vector.tensor_copy(T.ys[:, 0:HQ], T.poa[:, 0:HQ]).then_inc(sem.yc, 1)
    g.vector.wait_ge(sem.odb, 1)
    g.vector.tensor_copy(T.ys[:, HQ:QP], T.pob[:, 0:HQ]).then_inc(sem.yc, 1)
    g.sync.wait_ge(sem.yc, 2)
    g.sync.dma_start(T.y[:], T.ys[:]).then_inc(sem.st, 16)
    g.sync.wait_ge(sem.st, 16)
